import numpy as np, ml_dtypes
CORES = [2,3,42,43,82,83,122,123]
N = 8
DEG, TK, TIMES = 3, 128, 2
MASK = [[3,5,0],[3,5,1],[3,5,2],[3,5,0],[3,5,4],[3,5,0],[3,5,6],[3,5,7]]
def setup_inputs(rng):
    return {"x": rng.standard_normal((N, 128, TK), dtype=np.float32).astype(ml_dtypes.bfloat16), "w": (rng.standard_normal((N, 128, DEG * 128), dtype=np.float32) / np.float32(np.sqrt(128 * DEG / 2))).astype(ml_dtypes.bfloat16)}
def setup_inputs_big(rng):
    d = setup_inputs(rng)
    for k in ("x",): d[k] = (d[k].astype(np.float32) * 1048576.0).astype(d[k].dtype)
    return d
def setup_inputs_small(rng):
    d = setup_inputs(rng)
    for k in ("x",): d[k] = (d[k].astype(np.float32) * (1 / 1048576.0)).astype(d[k].dtype)
    return d
def setup_inputs_apart(rng):
    d = setup_inputs(rng)
    f = (10.0 ** rng.permutation(np.linspace(-1.5, 1.5, N))).astype(np.float32).reshape(N, 1, 1)
    for k in ("x",): d[k] = (d[k].astype(np.float32) * f).astype(d[k].dtype)
    return d
def reference(x, w):
    X, W = x.astype(np.float64), w.astype(np.float64)
    h = list(X)
    for _ in range(TIMES):
        h = [np.maximum(sum(W[r][:, 128 * i:128 * i + 128].T @ h[j] for i, j in enumerate(MASK[r])), 0.0) for r in range(N)]
    return {"y": np.stack(h).astype(ml_dtypes.bfloat16)}

@@ -1,0 +1,186 @@
+from concourse.bass import DstId, RemoteDMATransfer
+from concourse.mybir import AluOpType
+
+TK = 128
+DEG = 3
+NG = 3
+BW = TK * (1 + DEG)
+
+SCRATCH = {
+    "LG": ("sbuf", [128, NG * BW], "bfloat16"),
+    "LO": ("sbuf", [128, BW], "bfloat16"),
+    "HG": ("sbuf", [128, NG * TK], "bfloat16"),
+    "HO": ("sbuf", [128, TK], "bfloat16"),
+    "Y": ("sbuf", [128, TK], "bfloat16"),
+    "Z": ("sbuf", [128, TK], "float32"),
+    "P0": ("psum", [128, 512], "float32"),
+    "P1": ("psum", [128, 512], "float32"),
+    "P2": ("psum", [128, 512], "float32"),
+    "P3": ("psum", [128, 512], "float32"),
+}
+SEMAPHORES = ["ld", "z", "b0", "b1", "b2", "hg", "m0", "m1", "m2", "m3", "r0", "r1", "r2", "r3", "st", "sent"]
+
+
+def _bits(m):
+    return [b for b in range(m.bit_length()) if (m >> b) & 1]
+
+
+def _mask(bits):
+    return sum(1 << b for b in bits)
+
+
+def _plan(MASK, cores, topo):
+    n = len(MASK)
+    G = sorted({j for r in range(n) for j in MASK[r] if j != r})
+    if len(G) != NG or not all(k in G for j in G for k in MASK[j]):
+        raise ValueError("the ranks that are read must read only one another")
+    leaves = [r for r in range(n) if r not in G]
+    need = sorted({j for r in leaves for j in MASK[r] if j != r})
+
+    def hops(a, b):
+        ca, cb = topo.chip(cores[a]), topo.chip(cores[b])
+        if ca == cb:
+            return 0
+        return 1 if (topo.mates(ca, cb) or topo.same_plane(ca, cb)) else 2
+
+    serves = {j: [] for j in G}
+    for r in sorted(leaves, key=lambda r: min(hops(j, r) for j in G)):
+        j = min(G, key=lambda j: (hops(j, r) != 0, len(serves[j]), j not in need, hops(j, r)))
+        serves[j].append(r)
+
+    calls = {}
+    for k, j in enumerate(G):
+        c = cores[j]
+        away = [d for d in cores if topo.chip(d) != topo.chip(c)]
+        near = [d for d in cores if topo.chip(d) == topo.chip(c) and d != c]
+        low = _bits(topo.mask(c, away[0]))
+        high = [b for b in _bits(topo.mask(c, near[0])) if b not in low] if near else []
+
+        def split(dests):
+            on = [d for d in dests if hops(j, d) == 0]
+            off = [d for d in dests if hops(j, d) != 0]
+            if on and off and high:
+                return [(on, high), (off, low)]
+            return [(on + off, low)]
+
+        out = [("B", [([G[(k + d) % NG] for d in range(1, NG)], low)])]
+        if j in need:
+            out.append(("x", split([r for r in leaves if j in MASK[r]])))
+        if serves[j]:
+            out.append(("h", split(serves[j])))
+        for _, trs in out:
+            for dests, _b in trs:
+                for d in dests:
+                    if not topo.may_write(c, cores[d]):
+                        raise ValueError("core %d may not write to core %d" % (c, cores[d]))
+        calls[j] = out
+    inc = {}
+    for j in G:
+        for kind, trs in calls[j]:
+            for dests, bits in trs:
+                for d in dests:
+                    inc[("h" if kind == "h" else j, d)] = len(bits)
+    return G, need, calls, inc, hops
+
+
+def rank_program(g, core, T, topo):
+    r = T.rank_of(core)
+    if r is None:
+        return
+    MASK = T.tables["MASK"]
+    cores = list(T.cores)
+    S = T.sem
+    G, need, calls, inc, hops = _plan(MASK, cores, topo)
+    gi = {j: k for k, j in enumerate(G)}
+    in_g = r in gi
+    te, ve = g.tensor, g.vector
+    ps = [T.P0, T.P1, T.P2, T.P3]
+
+    def blk(j):
+        return (T.LO, 0) if (j == r and not in_g) else (T.LG, BW * gi[j])
+
+    def X(j):
+        t, o = blk(j)
+        return t[:, o:o + TK]
+
+    def W(j, i):
+        t, o = blk(j)
+        return t[:, o + TK * (1 + i):o + TK * (2 + i)]
+
+    def H(j):
+        return T.HO[:, 0:TK] if (j == r and not in_g) else T.HG[:, TK * gi[j]:TK * (gi[j] + 1)]
+
+    t, o = blk(r)
+    g.sync.dma_start(t[:, o:o + TK], T.x[:, :]).then_inc(S.ld, 16)
+    g.scalar.dma_start(t[:, o + TK:o + BW], T.w[:, :]).then_inc(S.ld, 16)
+    ve.memset(T.Z[:, :], 0.0).then_inc(S.z, 1)
+    ve.wait_ge(S.z, 1)
+
+    if in_g:
+        groups = need + [j for j in G if j not in need]
+        k = gi[r]
+        order = [r] + [G[(k - d) % NG] for d in range(1, NG)]
+    else:
+        groups = [r]
+        order = [r] + sorted({j for j in MASK[r] if j != r}, key=lambda j: hops(j, r))
+    pos = {j: p for p, j in enumerate(groups)}
+    stage = {j: s for s, j in enumerate(order)}
+    mms = sorted((max(stage[j], stage[MASK[j][i]]), pos[j], i, j) for j in groups for i in range(DEG))
+
+    te.wait_ge(S.ld, 32)
+    left = {j: DEG for j in groups}
+    begun, closed, waited = set(), [], 0
+    for s, p, i, j in mms:
+        while waited < s:
+            waited += 1
+            te.wait_ge(S["b%d" % gi[order[waited]]], inc[(order[waited], r)])
+        left[j] -= 1
+        ins = te.matmul(ps[p][:, 0:TK], W(j, i), X(MASK[j][i]), j not in begun, left[j] == 0)
+        begun.add(j)
+        if left[j] == 0:
+            ins.then_inc(S["m%d" % p], 1)
+            closed.append(j)
+    for j in closed:
+        ve.wait_ge(S["m%d" % pos[j]], 1)
+        ve.tensor_tensor(H(j), ps[pos[j]][:, 0:TK], T.Z[:, :], AluOpType.max).then_inc(S["r%d" % pos[j]], 1)
+
+    if in_g:
+        lo, hi = TK * min(gi[j] for j in need), TK * (max(gi[j] for j in need) + 1)
+        piece = {"B": T.LG[:, BW * gi[r]:BW * (gi[r] + 1)], "x": T.LG[:, BW * gi[r]:BW * gi[r] + TK],
+                 "h": T.HG[:, lo:hi]}
+        sent = 0
+        for kind, trs in calls[r]:
+            if kind == "B":
+                g.wait_ge(S.ld, 32)
+            if kind == "h":
+                for j in need:
+                    g.wait_ge(S["r%d" % pos[j]], 1)
+            fused = []
+            for dests, bits in trs:
+                ids = []
+                for d in dests:
+                    rid, pid, _se = topo.addr(cores[d])
+                    ids.append(DstId(rid=rid, pnc=pid))
+                fused.append(RemoteDMATransfer(dst_ids=ids, dma_engine_mask=_mask(bits),
+                                               remote_sem=S.hg if kind == "h" else S["b%d" % gi[r]],
+                                               srcs=[piece[kind]], dsts=[piece[kind] for _d in dests], alu_op=0))
+                sent += len(bits)
+            g.remote_dma_fused(fused, local_sem=S.sent)
+        g.wait_ge(S.sent, sent)
+
+    terms = sorted(range(DEG), key=lambda i: closed.index(MASK[r][i]) if MASK[r][i] in pos else len(closed))
+    landed = False
+    for n, i in enumerate(terms):
+        j = MASK[r][i]
+        if j in pos:
+            te.wait_ge(S["r%d" % pos[j]], 1)
+        elif not landed:
+            te.wait_ge(S.hg, inc[("h", r)])
+            landed = True
+        ins = te.matmul(ps[3][:, 0:TK], W(r, i), H(j), n == 0, n == DEG - 1)
+    ins.then_inc(S.m3, 1)
+    ve.wait_ge(S.m3, 1)
+    ve.tensor_tensor(T.Y[:, :], ps[3][:, 0:TK], T.Z[:, :], AluOpType.max).then_inc(S.r3, 1)
+    g.sync.wait_ge(S.r3, 1)
+    g.sync.dma_start(T.y[:, :], T.Y[:, :]).then_inc(S.st, 16)
+    g.sync.wait_ge(S.st, 16)

@@ -1,5 +1,5 @@
 from concourse.bass import DstId, RemoteDMATransfer
-from concourse.mybir import AluOpType
+from concourse.mybir import AluOpType, ActivationFunctionType
 
 TK = 128
 DEG = 3
@@ -15,10 +15,10 @@ SCRATCH = {
     "Z": ("sbuf", [128, TK], "float32"),
     "P0": ("psum", [128, 512], "float32"),
     "P1": ("psum", [128, 512], "float32"),
-    "P2": ("psum", [128, 512], "float32"),
     "P3": ("psum", [128, 512], "float32"),
 }
-SEMAPHORES = ["ld", "z", "b0", "b1", "b2", "hg", "m0", "m1", "m2", "m3", "r0", "r1", "r2", "r3", "st", "sent"]
+SEMAPHORES = ["lx", "lw", "z", "b0", "b1", "b2", "bw", "t0", "t1", "t2", "m0", "m1", "m3", "r0", "r1", "r3",
+              "st", "sent"]
 
 
 def _bits(m):
@@ -32,55 +32,58 @@ def _mask(bits):
 def _plan(MASK, cores, topo):
     n = len(MASK)
     G = sorted({j for r in range(n) for j in MASK[r] if j != r})
-    if len(G) != NG or not all(k in G for j in G for k in MASK[j]):
+    hubs = sorted({j for r in range(n) if r not in G for j in MASK[r] if j != r})
+    mids = [j for j in G if j not in hubs]
+    if len(G) != NG or len(hubs) != 2 or not all(k in G for j in G for k in MASK[j]):
         raise ValueError("the ranks that are read must read only one another")
-    leaves = [r for r in range(n) if r not in G]
-    need = sorted({j for r in leaves for j in MASK[r] if j != r})
+    made = {r: (hubs if r in hubs else [r]) for r in range(n)}
 
-    def hops(a, b):
+    def route(a, b):
         ca, cb = topo.chip(cores[a]), topo.chip(cores[b])
         if ca == cb:
             return 0
-        return 1 if (topo.mates(ca, cb) or topo.same_plane(ca, cb)) else 2
+        return 1 if topo.same_plane(ca, cb) else 2
 
-    serves = {j: [] for j in G}
-    for r in sorted(leaves, key=lambda r: min(hops(j, r) for j in G)):
-        j = min(G, key=lambda j: (hops(j, r) != 0, len(serves[j]), j not in need, hops(j, r)))
-        serves[j].append(r)
-
-    calls = {}
-    for k, j in enumerate(G):
-        c = cores[j]
+    def engines(a):
+        c = cores[a]
         away = [d for d in cores if topo.chip(d) != topo.chip(c)]
         near = [d for d in cores if topo.chip(d) == topo.chip(c) and d != c]
         low = _bits(topo.mask(c, away[0]))
-        high = [b for b in _bits(topo.mask(c, near[0])) if b not in low] if near else []
+        return low, [b for b in _bits(topo.mask(c, near[0])) if b not in low]
+
+    serves = {j: [] for j in hubs}
+    for r in sorted((r for r in range(n) if r not in hubs), key=lambda r: min(route(j, r) for j in hubs)):
+        serves[min(hubs, key=lambda j: (route(j, r), len(serves[j])))].append(r)
+
+    calls = {}
+    for j in G:
+        low, high = engines(j)
 
         def split(dests):
-            on = [d for d in dests if hops(j, d) == 0]
-            off = [d for d in dests if hops(j, d) != 0]
-            if on and off and high:
-                return [(on, high), (off, low)]
-            return [(on + off, low)]
+            return [([d for d in dests if route(j, d) != 0], low), ([d for d in dests if route(j, d) == 0], high)]
 
-        out = [("B", [([G[(k + d) % NG] for d in range(1, NG)], low)])]
-        if j in need:
-            out.append(("x", split([r for r in leaves if j in MASK[r]])))
-        if serves[j]:
-            out.append(("h", split(serves[j])))
-        for _, trs in out:
-            for dests, _b in trs:
-                for d in dests:
-                    if not topo.may_write(c, cores[d]):
-                        raise ValueError("core %d may not write to core %d" % (c, cores[d]))
-        calls[j] = out
+        xd = [r for r in range(n) if r != j and any(j in MASK[t] for t in made[r])]
+        if j in hubs:
+            p = [k for k in hubs if k != j][0]
+            on = [d for d in xd if route(j, d) == 0]
+            mid = [d for d in xd if route(j, d) != 0 and d in mids]
+            far = sorted((d for d in xd if route(j, d) != 0 and d not in mids and d != p), key=lambda d: route(j, d))
+            out = [("x", j, split([p])), ("W", j, split([p])), ("x", j, [(mid, low), (on, high)]),
+                   ("t", j, split(serves[j])), ("t", p, split(serves[j]))]
+            calls[on[0]] = [("f", j, [(far, engines(on[0])[0])])]
+        else:
+            out = [("x", j, split(xd)), ("t", j, split([r for r in range(n) if r != j and j in MASK[r]]))]
+        out = [(kind, s, [(d, b) for d, b in trs if d]) for kind, s, trs in out]
+        calls[j] = [(kind, s, trs) for kind, s, trs in out if trs]
     inc = {}
-    for j in G:
-        for kind, trs in calls[j]:
+    for a in calls:
+        for kind, s, trs in calls[a]:
             for dests, bits in trs:
                 for d in dests:
-                    inc[("h" if kind == "h" else j, d)] = len(bits)
-    return G, need, calls, inc, hops
+                    if not topo.may_write(cores[a], cores[d]):
+                        raise ValueError("core %d may not write to core %d" % (cores[a], cores[d]))
+                    inc[("x" if kind == "f" else kind, s, d)] = len(bits)
+    return G, hubs, mids, made, serves, calls, inc, route
 
 
 def rank_program(g, core, T, topo):
@@ -90,11 +93,11 @@ def rank_program(g, core, T, topo):
     MASK = T.tables["MASK"]
     cores = list(T.cores)
     S = T.sem
-    G, need, calls, inc, hops = _plan(MASK, cores, topo)
+    G, hubs, mids, made, serves, calls, inc, route = _plan(MASK, cores, topo)
     gi = {j: k for k, j in enumerate(G)}
     in_g = r in gi
     te, ve = g.tensor, g.vector
-    ps = [T.P0, T.P1, T.P2, T.P3]
+    ps = [T.P0, T.P1]
 
     def blk(j):
         return (T.LO, 0) if (j == r and not in_g) else (T.LG, BW * gi[j])
@@ -111,76 +114,83 @@ def rank_program(g, core, T, topo):
         return T.HO[:, 0:TK] if (j == r and not in_g) else T.HG[:, TK * gi[j]:TK * (gi[j] + 1)]
 
     t, o = blk(r)
-    g.sync.dma_start(t[:, o:o + TK], T.x[:, :]).then_inc(S.ld, 16)
-    g.scalar.dma_start(t[:, o + TK:o + BW], T.w[:, :]).then_inc(S.ld, 16)
+    g.sync.dma_start(t[:, o:o + TK], T.x[:, :]).then_inc(S.lx, 16)
+    g.scalar.dma_start(t[:, o + TK:o + BW], T.w[:, :]).then_inc(S.lw, 16)
     ve.memset(T.Z[:, :], 0.0).then_inc(S.z, 1)
     ve.wait_ge(S.z, 1)
 
-    if in_g:
-        groups = need + [j for j in G if j not in need]
-        k = gi[r]
-        order = [r] + [G[(k - d) % NG] for d in range(1, NG)]
-    else:
-        groups = [r]
-        order = [r] + sorted({j for j in MASK[r] if j != r}, key=lambda j: hops(j, r))
+    groups = [r] + [j for j in made[r] if j != r]
+    srcs = sorted({k for j in groups for k in MASK[j] if k != r}, key=lambda k: (k in mids, route(k, r)))
+    events = [("x", k) for k in srcs] + [("W", j) for j in groups if j != r]
+    sx, sw = {r: 0}, {r: 0}
+    for n, (kind, k) in enumerate(events):
+        (sx if kind == "x" else sw)[k] = n + 1
     pos = {j: p for p, j in enumerate(groups)}
-    stage = {j: s for s, j in enumerate(order)}
-    mms = sorted((max(stage[j], stage[MASK[j][i]]), pos[j], i, j) for j in groups for i in range(DEG))
+    mms = sorted((max(sw[j], sx[MASK[j][i]]), pos[j], i, j) for j in groups for i in range(DEG))
 
-    te.wait_ge(S.ld, 32)
+    te.wait_ge(S.lx, 16)
+    te.wait_ge(S.lw, 16)
     left = {j: DEG for j in groups}
-    begun, closed, waited = set(), [], 0
+    closed, waited = [], 0
     for s, p, i, j in mms:
         while waited < s:
+            kind, k = events[waited]
+            te.wait_ge(S.bw if kind == "W" else S["b%d" % gi[k]], inc[(kind, k, r)])
             waited += 1
-            te.wait_ge(S["b%d" % gi[order[waited]]], inc[(order[waited], r)])
         left[j] -= 1
-        ins = te.matmul(ps[p][:, 0:TK], W(j, i), X(MASK[j][i]), j not in begun, left[j] == 0)
-        begun.add(j)
+        ins = te.matmul(ps[p][:, 0:TK], W(j, i), X(MASK[j][i]), left[j] == DEG - 1, left[j] == 0)
         if left[j] == 0:
             ins.then_inc(S["m%d" % p], 1)
             closed.append(j)
-    for j in closed:
-        ve.wait_ge(S["m%d" % pos[j]], 1)
-        ve.tensor_tensor(H(j), ps[pos[j]][:, 0:TK], T.Z[:, :], AluOpType.max).then_inc(S["r%d" % pos[j]], 1)
+    for n, j in enumerate(closed):
+        p = pos[j]
+        if n % 2 == 0:
+            ve.wait_ge(S["m%d" % p], 1)
+            ve.tensor_tensor(H(j), ps[p][:, 0:TK], T.Z[:, :], AluOpType.max).then_inc(S["r%d" % p], 1)
+        else:
+            g.scalar.wait_ge(S["m%d" % p], 1)
+            g.scalar.activation(H(j), ps[p][:, 0:TK], ActivationFunctionType.Relu).then_inc(S["r%d" % p], 1)
 
-    if in_g:
-        lo, hi = TK * min(gi[j] for j in need), TK * (max(gi[j] for j in need) + 1)
-        piece = {"B": T.LG[:, BW * gi[r]:BW * (gi[r] + 1)], "x": T.LG[:, BW * gi[r]:BW * gi[r] + TK],
-                 "h": T.HG[:, lo:hi]}
+    if r in calls:
         sent = 0
-        for kind, trs in calls[r]:
-            if kind == "B":
-                g.wait_ge(S.ld, 32)
-            if kind == "h":
-                for j in need:
-                    g.wait_ge(S["r%d" % pos[j]], 1)
+        for kind, s, trs in calls[r]:
+            k = gi[s]
+            if kind == "x":
+                g.wait_ge(S.lx, 16)
+            if kind == "W":
+                g.wait_ge(S.lw, 16)
+            if kind == "f":
+                g.wait_ge(S["b%d" % k], inc[("x", s, r)])
+            if kind == "t":
+                g.wait_ge(S["r%d" % pos[s]], 1)
+            piece = (T.LG[:, BW * k + TK:BW * (k + 1)] if kind == "W" else
+                     T.HG[:, TK * k:TK * (k + 1)] if kind == "t" else T.LG[:, BW * k:BW * k + TK])
+            rsem = S.bw if kind == "W" else S["t%d" % k] if kind == "t" else S["b%d" % k]
             fused = []
             for dests, bits in trs:
                 ids = []
                 for d in dests:
                     rid, pid, _se = topo.addr(cores[d])
                     ids.append(DstId(rid=rid, pnc=pid))
-                fused.append(RemoteDMATransfer(dst_ids=ids, dma_engine_mask=_mask(bits),
-                                               remote_sem=S.hg if kind == "h" else S["b%d" % gi[r]],
-                                               srcs=[piece[kind]], dsts=[piece[kind] for _d in dests], alu_op=0))
+                fused.append(RemoteDMATransfer(dst_ids=ids, dma_engine_mask=_mask(bits), remote_sem=rsem,
+                                               srcs=[piece], dsts=[piece for _d in dests], alu_op=0))
                 sent += len(bits)
             g.remote_dma_fused(fused, local_sem=S.sent)
         g.wait_ge(S.sent, sent)
 
-    terms = sorted(range(DEG), key=lambda i: closed.index(MASK[r][i]) if MASK[r][i] in pos else len(closed))
-    landed = False
+    near = [j for j in hubs if r in serves[j]]
+    terms = sorted(range(DEG), key=lambda i: (0, closed.index(MASK[r][i])) if MASK[r][i] in pos
+                   else (1, MASK[r][i] not in near))
     for n, i in enumerate(terms):
         j = MASK[r][i]
         if j in pos:
             te.wait_ge(S["r%d" % pos[j]], 1)
-        elif not landed:
-            te.wait_ge(S.hg, inc[("h", r)])
-            landed = True
-        ins = te.matmul(ps[3][:, 0:TK], W(r, i), H(j), n == 0, n == DEG - 1)
+        else:
+            te.wait_ge(S["t%d" % gi[j]], inc[("t", j, r)])
+        ins = te.matmul(T.P3[:, 0:TK], W(r, i), H(j), n == 0, n == DEG - 1)
     ins.then_inc(S.m3, 1)
     ve.wait_ge(S.m3, 1)
-    ve.tensor_tensor(T.Y[:, :], ps[3][:, 0:TK], T.Z[:, :], AluOpType.max).then_inc(S.r3, 1)
+    ve.tensor_tensor(T.Y[:, :], T.P3[:, 0:TK], T.Z[:, :], AluOpType.max).then_inc(S.r3, 1)
     g.sync.wait_ge(S.r3, 1)
     g.sync.dma_start(T.y[:, :], T.Y[:, :]).then_inc(S.st, 16)
     g.sync.wait_ge(S.st, 16)

from concourse.bass import DstId, RemoteDMATransfer
from concourse.mybir import AluOpType, ActivationFunctionType

TK = 128
DEG = 3
NG = 3
BW = TK * (1 + DEG)

SCRATCH = {
    "LG": ("sbuf", [128, NG * BW], "bfloat16"),
    "LO": ("sbuf", [128, BW], "bfloat16"),
    "HG": ("sbuf", [128, NG * TK], "bfloat16"),
    "HO": ("sbuf", [128, TK], "bfloat16"),
    "Y": ("sbuf", [128, TK], "bfloat16"),
    "Z": ("sbuf", [128, TK], "float32"),
    "P0": ("psum", [128, 512], "float32"),
    "P1": ("psum", [128, 512], "float32"),
    "P3": ("psum", [128, 512], "float32"),
}
SEMAPHORES = ["lx", "lw", "z", "b0", "b1", "b2", "bw", "t0", "t1", "t2", "m0", "m1", "m3", "r0", "r1", "r3",
              "st", "sent"]


def _bits(m):
    return [b for b in range(m.bit_length()) if (m >> b) & 1]


def _mask(bits):
    return sum(1 << b for b in bits)


def _plan(MASK, cores, topo):
    n = len(MASK)
    G = sorted({j for r in range(n) for j in MASK[r] if j != r})
    hubs = sorted({j for r in range(n) if r not in G for j in MASK[r] if j != r})
    mids = [j for j in G if j not in hubs]
    if len(G) != NG or len(hubs) != 2 or not all(k in G for j in G for k in MASK[j]):
        raise ValueError("the ranks that are read must read only one another")
    made = {r: (hubs if r in hubs else [r]) for r in range(n)}

    def route(a, b):
        ca, cb = topo.chip(cores[a]), topo.chip(cores[b])
        if ca == cb:
            return 0
        return 1 if topo.same_plane(ca, cb) else 2

    def engines(a):
        c = cores[a]
        away = [d for d in cores if topo.chip(d) != topo.chip(c)]
        near = [d for d in cores if topo.chip(d) == topo.chip(c) and d != c]
        low = _bits(topo.mask(c, away[0]))
        return low, [b for b in _bits(topo.mask(c, near[0])) if b not in low]

    serves = {j: [] for j in hubs}
    for r in sorted((r for r in range(n) if r not in hubs), key=lambda r: min(route(j, r) for j in hubs)):
        serves[min(hubs, key=lambda j: (route(j, r), len(serves[j])))].append(r)

    calls = {}
    for j in G:
        low, high = engines(j)

        def split(dests):
            return [([d for d in dests if route(j, d) != 0], low), ([d for d in dests if route(j, d) == 0], high)]

        xd = [r for r in range(n) if r != j and any(j in MASK[t] for t in made[r])]
        if j in hubs:
            p = [k for k in hubs if k != j][0]
            on = [d for d in xd if route(j, d) == 0]
            mid = [d for d in xd if route(j, d) != 0 and d in mids]
            far = sorted((d for d in xd if route(j, d) != 0 and d not in mids and d != p), key=lambda d: route(j, d))
            out = [("x", j, split([p])), ("W", j, split([p])), ("x", j, [(mid, low), (on, high)]),
                   ("t", j, split(serves[j])), ("t", p, split(serves[j]))]
            calls[on[0]] = [("f", j, [(far, engines(on[0])[0])])]
        else:
            out = [("x", j, split(xd)), ("t", j, split([r for r in range(n) if r != j and j in MASK[r]]))]
        out = [(kind, s, [(d, b) for d, b in trs if d]) for kind, s, trs in out]
        calls[j] = [(kind, s, trs) for kind, s, trs in out if trs]
    inc = {}
    for a in calls:
        for kind, s, trs in calls[a]:
            for dests, bits in trs:
                for d in dests:
                    if not topo.may_write(cores[a], cores[d]):
                        raise ValueError("core %d may not write to core %d" % (cores[a], cores[d]))
                    inc[("x" if kind == "f" else kind, s, d)] = len(bits)
    return G, hubs, mids, made, serves, calls, inc, route


def rank_program(g, core, T, topo):
    r = T.rank_of(core)
    if r is None:
        return
    MASK = T.tables["MASK"]
    cores = list(T.cores)
    S = T.sem
    G, hubs, mids, made, serves, calls, inc, route = _plan(MASK, cores, topo)
    gi = {j: k for k, j in enumerate(G)}
    in_g = r in gi
    te, ve = g.tensor, g.vector
    ps = [T.P0, T.P1]

    def blk(j):
        return (T.LO, 0) if (j == r and not in_g) else (T.LG, BW * gi[j])

    def X(j):
        t, o = blk(j)
        return t[:, o:o + TK]

    def W(j, i):
        t, o = blk(j)
        return t[:, o + TK * (1 + i):o + TK * (2 + i)]

    def H(j):
        return T.HO[:, 0:TK] if (j == r and not in_g) else T.HG[:, TK * gi[j]:TK * (gi[j] + 1)]

    t, o = blk(r)
    g.sync.dma_start(t[:, o:o + TK], T.x[:, :]).then_inc(S.lx, 16)
    g.scalar.dma_start(t[:, o + TK:o + BW], T.w[:, :]).then_inc(S.lw, 16)
    ve.memset(T.Z[:, :], 0.0).then_inc(S.z, 1)
    ve.wait_ge(S.z, 1)

    groups = [r] + [j for j in made[r] if j != r]
    srcs = sorted({k for j in groups for k in MASK[j] if k != r}, key=lambda k: (k in mids, route(k, r)))
    events = [("x", k) for k in srcs] + [("W", j) for j in groups if j != r]
    sx, sw = {r: 0}, {r: 0}
    for n, (kind, k) in enumerate(events):
        (sx if kind == "x" else sw)[k] = n + 1
    pos = {j: p for p, j in enumerate(groups)}
    mms = sorted((max(sw[j], sx[MASK[j][i]]), pos[j], i, j) for j in groups for i in range(DEG))

    te.wait_ge(S.lx, 16)
    te.wait_ge(S.lw, 16)
    left = {j: DEG for j in groups}
    closed, waited = [], 0
    for s, p, i, j in mms:
        while waited < s:
            kind, k = events[waited]
            te.wait_ge(S.bw if kind == "W" else S["b%d" % gi[k]], inc[(kind, k, r)])
            waited += 1
        left[j] -= 1
        ins = te.matmul(ps[p][:, 0:TK], W(j, i), X(MASK[j][i]), left[j] == DEG - 1, left[j] == 0)
        if left[j] == 0:
            ins.then_inc(S["m%d" % p], 1)
            closed.append(j)
    for n, j in enumerate(closed):
        p = pos[j]
        if n % 2 == 0:
            ve.wait_ge(S["m%d" % p], 1)
            ve.tensor_tensor(H(j), ps[p][:, 0:TK], T.Z[:, :], AluOpType.max).then_inc(S["r%d" % p], 1)
        else:
            g.scalar.wait_ge(S["m%d" % p], 1)
            g.scalar.activation(H(j), ps[p][:, 0:TK], ActivationFunctionType.Relu).then_inc(S["r%d" % p], 1)

    if r in calls:
        sent = 0
        for kind, s, trs in calls[r]:
            k = gi[s]
            if kind == "x":
                g.wait_ge(S.lx, 16)
            if kind == "W":
                g.wait_ge(S.lw, 16)
            if kind == "f":
                g.wait_ge(S["b%d" % k], inc[("x", s, r)])
            if kind == "t":
                g.wait_ge(S["r%d" % pos[s]], 1)
            piece = (T.LG[:, BW * k + TK:BW * (k + 1)] if kind == "W" else
                     T.HG[:, TK * k:TK * (k + 1)] if kind == "t" else T.LG[:, BW * k:BW * k + TK])
            rsem = S.bw if kind == "W" else S["t%d" % k] if kind == "t" else S["b%d" % k]
            fused = []
            for dests, bits in trs:
                ids = []
                for d in dests:
                    rid, pid, _se = topo.addr(cores[d])
                    ids.append(DstId(rid=rid, pnc=pid))
                fused.append(RemoteDMATransfer(dst_ids=ids, dma_engine_mask=_mask(bits), remote_sem=rsem,
                                               srcs=[piece], dsts=[piece for _d in dests], alu_op=0))
                sent += len(bits)
            g.remote_dma_fused(fused, local_sem=S.sent)
        g.wait_ge(S.sent, sent)

    near = [j for j in hubs if r in serves[j]]
    terms = sorted(range(DEG), key=lambda i: (0, closed.index(MASK[r][i])) if MASK[r][i] in pos
                   else (1, MASK[r][i] not in near))
    for n, i in enumerate(terms):
        j = MASK[r][i]
        if j in pos:
            te.wait_ge(S["r%d" % pos[j]], 1)
        else:
            te.wait_ge(S["t%d" % gi[j]], inc[("t", j, r)])
        ins = te.matmul(T.P3[:, 0:TK], W(r, i), H(j), n == 0, n == DEG - 1)
    ins.then_inc(S.m3, 1)
    ve.wait_ge(S.m3, 1)
    ve.tensor_tensor(T.Y[:, :], T.P3[:, 0:TK], T.Z[:, :], AluOpType.max).then_inc(S.r3, 1)
    g.sync.wait_ge(S.r3, 1)
    g.sync.dma_start(T.y[:, :], T.Y[:, :]).then_inc(S.st, 16)
    g.sync.wait_ge(S.st, 16)
